import numpy as np
import ml_dtypes


def mxq(x, axis, fmt="e4m3"):
    dtype, down = {"e4m3": (ml_dtypes.float8_e4m3fn, 7), "e5m2": (ml_dtypes.float8_e5m2, 14)}[fmt]
    v = np.moveaxis(np.asarray(x, np.float32).astype(ml_dtypes.bfloat16).astype(np.float64), axis, -1)
    blocks = v.reshape(v.shape[:-1] + (-1, 32))
    amax = np.abs(blocks).max(-1, keepdims=True)
    byte = np.maximum(np.where(amax > 0, np.frexp(amax)[1] - 1 + 127, 0) - down, 1)
    scale = np.exp2(byte - 127.0)
    codes = (blocks / scale).astype(np.float32).astype(dtype).astype(np.float64)
    return np.moveaxis((codes * scale).reshape(v.shape), -1, axis)


WIDE = False


def mx_kscale(k):
    if not WIDE:
        return np.ones(k)
    levels = np.array([10, -10, 5, -5, 0])
    if k % 512:
        return np.exp2(np.random.permutation(np.resize(levels, k // 32))).repeat(32)
    a = np.empty((k // 512, 16))
    for p in range(k // 512):
        a[p, :8] = np.random.permutation(np.resize(levels, 8))
        for g in range(8):
            far = levels[np.abs(levels - a[p, g]) >= 10]
            a[p, g + 8] = far[np.random.randint(len(far))]
    return np.exp2(a.ravel()).repeat(32)


def f64(x):
    return np.asarray(x).astype(np.float64)


def striped(idx):
    return np.tile(idx.reshape(-1, 16).T, (8, 1)).astype(np.uint16)


def unstriped(offs):
    return offs[:16].T.reshape(-1).astype(np.int64)


E2M1 = np.array([0.0, 0.5, 1.0, 1.5, 2.0, 3.0, 4.0, 6.0, -0.0, -0.5, -1.0, -1.5, -2.0, -3.0, -4.0, -6.0])


def pack_weight(w, fmt):
    k, n = w.shape
    w = f64(np.asarray(w, np.float32).astype(ml_dtypes.bfloat16)).reshape(k // 32, 32, n)
    amax = np.abs(w).max(1)
    if fmt == "e4m3":
        byte = np.frexp(amax)[1] - 1 + 127 - 7
    else:
        mant, ex = np.frexp(amax / 6.0)
        byte = np.where(mant > 0.5, ex, ex - 1) + 127
    byte = np.clip(np.where(amax > 0, byte, 1), 1, 254)
    scaled = (w * np.exp2(127.0 - byte)[:, None, :]).reshape(k, n).astype(np.float32)
    by_word = np.ascontiguousarray(scaled.reshape(k // 512, 128, 4, n).transpose(0, 1, 3, 2))
    if fmt == "e4m3":
        words = by_word.astype(ml_dtypes.float8_e4m3fn).view(np.uint8)
    else:
        c = by_word.astype(ml_dtypes.float4_e2m1fn).view(np.uint8) & 0xF
        words = (c[..., 0::2] | (c[..., 1::2] << 4)).reshape(k // 512, 128, 2 * n)
    return np.ascontiguousarray(words), np.ascontiguousarray(byte.astype(np.uint8).reshape(k // 512, 16, n))


def unpack_weight(words, scales, fmt):
    g, _, n = scales.shape
    words = np.ascontiguousarray(words).reshape(g, 128, n, -1)
    if fmt == "e4m3":
        vals = words.view(ml_dtypes.float8_e4m3fn).astype(np.float64)
    else:
        nib = np.empty((g, 128, n, 4), np.uint8)
        nib[..., 0::2] = words & 0xF
        nib[..., 1::2] = words >> 4
        vals = E2M1[nib]
    vals = vals * np.repeat(np.exp2(scales.astype(np.float64) - 127.0), 8, axis=1)[..., None]
    return vals.transpose(0, 1, 3, 2).reshape(g * 512, n)


def silu(v):
    return v / (1.0 + np.exp(-np.maximum(v, -700.0)))


K, T, E, C, H, N = 512, 768, 12, 128, 512, 128


def by_expert(wq, xq):
    return np.concatenate([wq[e].T @ xq[:, e * C:(e + 1) * C] for e in range(E)], axis=1)


def setup_inputs():
    n = np.random.standard_normal
    s = mx_kscale(K)[:, None]
    u = mx_kscale(H)
    first = np.random.permutation(np.repeat(np.arange(E), T // E))
    second = (first + 1 + np.random.permutation(np.repeat(np.arange(E - 1), -(-T // (E - 1)))[:T])) % E
    while np.bincount(second, minlength=E).max() != T // E:
        load = np.bincount(second, minlength=E); hi, lo = int(load.argmax()), int(load.argmin())
        t = np.flatnonzero((second == hi) & (first != lo))[0]; second[t] = lo
    slot_token = np.empty(E * C, np.int64); pos = np.empty((2, T), np.int64); fill = np.zeros(E, np.int64)
    place = np.stack([np.random.permutation(C) for _ in range(E)])
    for r, deal in enumerate((first, second)):
        for t in np.random.permutation(T):
            e = deal[t]; j = e * C + place[e, fill[e]]; fill[e] += 1; slot_token[j] = t; pos[r, t] = j
    g = np.random.uniform(0.2, 0.8, T)
    x = pack_weight(n((K, T)) * s, "e4m3")
    return {
        "x_words": x[0],
        "x_scales": x[1],
        "w1": (n((E, K, H)) / np.sqrt(K) / s[None] * u[None, None, :]).astype(np.float32),
        "w2": (n((E, H, N)) / np.sqrt(H) / u[None, :, None]).astype(np.float32),
        "gate": np.stack([np.tile(g, (N, 1)), np.tile(1.0 - g, (N, 1))]).astype(np.float32),
        "offs": striped(slot_token),
        "pos1": striped(pos[0]),
        "pos2": striped(pos[1]),
    }


def reference(x_words, x_scales, w1, w2, gate, offs, pos1, pos2):
    idx = unstriped(offs)
    xq = unpack_weight(x_words, x_scales, "e4m3")[:, idx]
    h = silu(by_expert(mxq(f64(w1), 1, "e4m3"), xq))
    y = by_expert(mxq(f64(w2), 1, "e4m3"), mxq(h, 0, "e4m3"))
    return f64(gate[0]) * y[:, unstriped(pos1)] + f64(gate[1]) * y[:, unstriped(pos2)]

@@ -1,0 +1,190 @@
+from contextlib import ExitStack
+
+import concourse.mybir as mybir
+
+K, T, E, C, H, N = 512, 768, 12, 128, 512, 128
+S = E * C
+P = 128
+FLOPS = 2 * S * (K * H + H * N)
+
+F32 = mybir.dt.float32
+BF16 = mybir.dt.bfloat16
+I32 = mybir.dt.int32
+U32 = mybir.dt.uint32
+U16 = mybir.dt.uint16
+U8 = mybir.dt.uint8
+FP8X4 = mybir.dt.float8_e4m3fn_x4
+ACT = mybir.ActivationFunctionType
+ALU = mybir.AluOpType
+
+PAIR = 2
+OUT_CHUNK = 256
+
+
+def tile_moe_pkd_mlp_silu_kernel(tc, x_words, x_scales, w1, w2, gate, offs, pos1, pos2, out):
+    nc = tc.nc
+    with ExitStack() as ctx:
+        keep = ctx.enter_context(tc.tile_pool(name="keep", bufs=1))
+        ring = ctx.enter_context(tc.tile_pool(name="ring", bufs=3))
+        gring = ctx.enter_context(tc.tile_pool(name="gring", bufs=2))
+        psum = ctx.enter_context(tc.psum_pool(name="psum", bufs=4))
+
+        offs_sb = keep.tile([P, S // 16], U16, name="offs_sb")
+        pos1_sb = keep.tile([P, T // 16], U16, name="pos1_sb")
+        pos2_sb = keep.tile([P, T // 16], U16, name="pos2_sb")
+        xw = keep.tile([P, T], I32, name="xw", align_bytes=64)
+        xs = keep.tile([P, T], U8, name="xs", align_bytes=64)
+        warm = keep.tile([P, 8], F32, name="warm")
+        warm_out = keep.tile([P, 8], F32, name="warm_out")
+        nc.gpsimd.memset(warm[:], 0.0)
+        nc.scalar.activation(out=warm_out[:], in_=warm[:], func=ACT.Silu)
+
+        nc.sync.dma_start(offs_sb[:], offs)
+        nc.sync.dma_start(xw[:], x_words[0].rearrange("p t r -> p (t r)").bitcast(I32))
+        rows = x_scales[0].bitcast(I32)
+        for q in range(4):
+            nc.sync.dma_start(
+                xs[32 * q : 32 * q + 32, :].bitcast(I32),
+                rows[4 * q : 4 * q + 4, :].unsqueeze(0).to_broadcast([8, 4, T // 4]),
+            )
+
+        w1_raw = [keep.tile([P, 4, H], F32, name="w1_raw%d" % e, align_bytes=64) for e in range(E)]
+        w2_raw = [keep.tile([P, 4, N], F32, name="w2_raw%d" % e) for e in range(E)]
+        gate_sb = [keep.tile([P, T], F32, name="gate_sb%d" % r) for r in range(2)]
+        LAG = 1
+        AHEAD = 2
+
+        for e in range(E + LAG):
+            if e < E:
+                nc.sync.dma_start(w1_raw[e][:], w1[e].rearrange("(p j) c -> p j c", j=4))
+            if e >= LAG:
+                nc.sync.dma_start(w2_raw[e - LAG][:], w2[e - LAG].rearrange("(p j) n -> p j n", j=4))
+            if e == 4:
+                nc.sync.dma_start(pos1_sb[:], pos1)
+                nc.sync.dma_start(pos2_sb[:], pos2)
+        for r in range(2):
+            nc.sync.dma_start(gate_sb[r][:], gate[r])
+
+        gw, gs = {}, {}
+        y = keep.tile([P, S], F32, name="y")
+        st = {}
+
+        def gather(g):
+            cols = slice(g * PAIR * C // 16, (g + 1) * PAIR * C // 16)
+            gw[g] = gring.tile([P, PAIR * C], U32, name="gw", align_bytes=64)
+            gs[g] = gring.tile([P, PAIR * C], U8, name="gs", align_bytes=64)
+            nc.vector.tensor_copy(gw[g][:], xw[:].bitcast(U32).indirect(offs_sb[:, cols]))
+            nc.vector.tensor_copy(gs[g][:], xs[:].indirect(offs_sb[:, cols]))
+
+        def cast_w1(e):
+            b = ring.tile([P, 4 * H], BF16, name="w1_bf", align_bytes=64)
+            dst = b[:].rearrange("p (t m j) -> p m j t", t=4, j=4)
+            src = w1_raw[e][:].rearrange("p j (m t) -> p m j t", t=4)
+            if e == E - 1:
+                nc.vector.tensor_copy(dst[:, :, :, 0:2], src[:, :, :, 0:2])
+                nc.scalar.copy(dst[:, :, :, 2:4], src[:, :, :, 2:4])
+            elif e % 2 == 1:
+                nc.vector.tensor_copy(dst, src)
+            else:
+                nc.scalar.copy(dst, src)
+            st["w1b", e] = b
+
+        def quant_w1(e):
+            q = ring.tile([P, H], U32, name="w1_q", align_bytes=64)
+            s = ring.tile([P, H], U8, name="w1_s", align_bytes=64)
+            parts = 2 if e == E - 1 else 1
+            w = H // parts
+            for i in range(parts):
+                nc.vector.quantize_mx(
+                    out=q[:, i * w : (i + 1) * w].bitcast(FP8X4),
+                    scales=s[:, i * w : (i + 1) * w],
+                    in_=st["w1b", e][:, 4 * i * w : 4 * (i + 1) * w],
+                )
+            st["w1q", e] = (q, s)
+
+        def layer1(e):
+            q, s = st["w1q", e]
+            slots = slice((e % PAIR) * C, (e % PAIR + 1) * C)
+            a = psum.tile([P, 4, C], F32, name="a")
+            for t in range(4):
+                nc.tensor.matmul_mx(
+                    out=a[:, t, :],
+                    lhsT=q[:, t * P : (t + 1) * P].bitcast(FP8X4),
+                    lhsT_scale=s[:, t * P : (t + 1) * P],
+                    rhs=gw[e // PAIR][:, slots].bitcast(FP8X4),
+                    rhs_scale=gs[e // PAIR][:, slots],
+                    start=True,
+                    stop=True,
+                )
+            st["a", e] = a
+
+        def stage2(e):
+            host = min(e + 2 - e % 2, E - 2)
+            b = w1_raw[host][:, e - host + 2, :].bitcast(BF16)
+            nc.scalar.activation(
+                out=b[:, 0 : 4 * C].rearrange("p (s t) -> p s t", t=4), in_=st["a", e][:].rearrange("p t s -> p s t"), func=ACT.Silu
+            )
+            dst = b[:, 4 * C :].rearrange("p (c i j) -> p c j i", i=4, j=4)
+            src = w2_raw[e][:].rearrange("p j (c i) -> p c j i", i=4)
+            if e in (10, 11):
+                nc.vector.tensor_copy(dst, src)
+            else:
+                nc.scalar.copy(dst, src)
+            st["b2", e] = b
+
+        def layer2(e):
+            q = ring.tile([P, C + N], U32, name="l2_q", align_bytes=64)
+            s = ring.tile([P, C + N], U8, name="l2_s", align_bytes=64)
+            nc.vector.quantize_mx(out=q[:].bitcast(FP8X4), scales=s[:], in_=st["b2", e])
+            if e % PAIR == 0:
+                st["yp"] = psum.tile([P, PAIR * C], F32, name="yp")
+            nc.tensor.matmul_mx(
+                out=st["yp"][:, (e % PAIR) * C : (e % PAIR + 1) * C],
+                lhsT=q[:, C:].bitcast(FP8X4),
+                lhsT_scale=s[:, C:],
+                rhs=q[:, :C].bitcast(FP8X4),
+                rhs_scale=s[:, :C],
+                start=True,
+                stop=True,
+            )
+            st["yp", e // PAIR] = st["yp"]
+
+        def y_out(g):
+            nc.vector.tensor_copy(y[:, g * PAIR * C : (g + 1) * PAIR * C], st["yp", g][:])
+
+        for g in range(AHEAD):
+            gather(g)
+        for g in range(E // PAIR + 1):
+            e0, e1 = PAIR * g, PAIR * g + 1
+            if e0 < E:
+                cast_w1(e0)
+            if g >= 2:
+                y_out(g - 2)
+            if g >= 1:
+                stage2(e0 - 2)
+                stage2(e0 - 1)
+            if e0 < E:
+                quant_w1(e0)
+                layer1(e0)
+                cast_w1(e1)
+            if g >= 1:
+                layer2(e0 - 2)
+            if e0 < E:
+                quant_w1(e1)
+                layer1(e1)
+            if g >= 1:
+                layer2(e0 - 1)
+            if g + AHEAD < E // PAIR:
+                gather(g + AHEAD)
+        y_out(E // PAIR - 1)
+
+        for c in range(T // OUT_CHUNK):
+            tok = slice(c * OUT_CHUNK, (c + 1) * OUT_CHUNK)
+            cols = slice(c * OUT_CHUNK // 16, (c + 1) * OUT_CHUNK // 16)
+            pa = ring.tile([P, OUT_CHUNK], F32, name="pa")
+            pb = ring.tile([P, OUT_CHUNK], F32, name="pb")
+            po = ring.tile([P, OUT_CHUNK], F32, name="po")
+            nc.vector.tensor_tensor(pa[:], y[:].indirect(pos1_sb[:, cols]), gate_sb[0][:, tok], ALU.mult)
+            nc.vector.tensor_tensor(pb[:], y[:].indirect(pos2_sb[:, cols]), gate_sb[1][:, tok], ALU.mult)
+            nc.vector.tensor_tensor(po[:], pa[:], pb[:], ALU.add)
+            nc.sync.dma_start(out[:, tok], po[:])

@@ -17,16 +17,19 @@ FP8X4 = mybir.dt.float8_e4m3fn_x4
 ACT = mybir.ActivationFunctionType
 ALU = mybir.AluOpType
 
-PAIR = 2
-OUT_CHUNK = 256
+GATHER = 512
+W2_GROUPS = (2, 2, 2, 2, 2, 1, 1)
+W2_VECTOR = (2, 2, 2, 0, 0, 1, 1)
+SHARED = 2
+Y_STARTS = (0, 4, 8, 11)
+OUT_CHUNKS = (512, 256)
 
 
 def tile_moe_pkd_mlp_silu_kernel(tc, x_words, x_scales, w1, w2, gate, offs, pos1, pos2, out):
     nc = tc.nc
     with ExitStack() as ctx:
         keep = ctx.enter_context(tc.tile_pool(name="keep", bufs=1))
-        ring = ctx.enter_context(tc.tile_pool(name="ring", bufs=3))
-        gring = ctx.enter_context(tc.tile_pool(name="gring", bufs=2))
+        ring = ctx.enter_context(tc.tile_pool(name="ring", bufs=4))
         psum = ctx.enter_context(tc.psum_pool(name="psum", bufs=4))
 
         offs_sb = keep.tile([P, S // 16], U16, name="offs_sb")
@@ -48,51 +51,52 @@ def tile_moe_pkd_mlp_silu_kernel(tc, x_words, x_scales, w1, w2, gate, offs, pos1
                 rows[4 * q : 4 * q + 4, :].unsqueeze(0).to_broadcast([8, 4, T // 4]),
             )
 
+        starts = [sum(W2_GROUPS[:g]) for g in range(len(W2_GROUPS))]
         w1_raw = [keep.tile([P, 4, H], F32, name="w1_raw%d" % e, align_bytes=64) for e in range(E)]
-        w2_raw = [keep.tile([P, 4, N], F32, name="w2_raw%d" % e) for e in range(E)]
-        gate_sb = [keep.tile([P, T], F32, name="gate_sb%d" % r) for r in range(2)]
-        LAG = 1
-        AHEAD = 2
+        w2_raw = [
+            keep.tile([P, z, 4, N], F32, name="w2_raw%d" % g, tag="w2_raw%d" % g, align_bytes=64) for g, z in enumerate(W2_GROUPS)
+        ]
+        gate_sb = [keep.tile([P, 2, w], F32, name="gate_sb%d" % i) for i, w in enumerate(OUT_CHUNKS)]
 
-        for e in range(E + LAG):
-            if e < E:
-                nc.sync.dma_start(w1_raw[e][:], w1[e].rearrange("(p j) c -> p j c", j=4))
-            if e >= LAG:
-                nc.sync.dma_start(w2_raw[e - LAG][:], w2[e - LAG].rearrange("(p j) n -> p j n", j=4))
+        for e in range(E):
+            nc.sync.dma_start(w1_raw[e][:], w1[e].rearrange("(p j) c -> p j c", j=4))
             if e == 4:
                 nc.sync.dma_start(pos1_sb[:], pos1)
                 nc.sync.dma_start(pos2_sb[:], pos2)
-        for r in range(2):
-            nc.sync.dma_start(gate_sb[r][:], gate[r])
+        for g, z in enumerate(W2_GROUPS):
+            nc.sync.dma_start(w2_raw[g][:], w2[starts[g] : starts[g] + z].rearrange("e (p j) n -> p e j n", j=4))
+        for i, w in enumerate(OUT_CHUNKS):
+            t0 = sum(OUT_CHUNKS[:i])
+            nc.sync.dma_start(gate_sb[i][:], gate[:, :, t0 : t0 + w].rearrange("r p t -> p r t"))
 
-        gw, gs = {}, {}
-        y = keep.tile([P, S], F32, name="y")
+        gw = [keep.tile([P, GATHER], U32, name="gw%d" % g, align_bytes=64) for g in range(S // GATHER)]
+        gs = [keep.tile([P, GATHER], U8, name="gs%d" % g, align_bytes=64) for g in range(S // GATHER)]
+        hq = [keep.tile([P, 2 * C], U32, name="hq%d" % g, align_bytes=64) for g in range(E // 2)]
+        hs = [keep.tile([P, 2 * C], U8, name="hs%d" % g, align_bytes=64) for g in range(E // 2)]
         st = {}
 
         def gather(g):
-            cols = slice(g * PAIR * C // 16, (g + 1) * PAIR * C // 16)
-            gw[g] = gring.tile([P, PAIR * C], U32, name="gw", align_bytes=64)
-            gs[g] = gring.tile([P, PAIR * C], U8, name="gs", align_bytes=64)
+            cols = slice(g * GATHER // 16, (g + 1) * GATHER // 16)
             nc.vector.tensor_copy(gw[g][:], xw[:].bitcast(U32).indirect(offs_sb[:, cols]))
             nc.vector.tensor_copy(gs[g][:], xs[:].indirect(offs_sb[:, cols]))
 
         def cast_w1(e):
             b = ring.tile([P, 4 * H], BF16, name="w1_bf", align_bytes=64)
-            dst = b[:].rearrange("p (t m j) -> p m j t", t=4, j=4)
-            src = w1_raw[e][:].rearrange("p j (m t) -> p m j t", t=4)
-            if e == E - 1:
-                nc.vector.tensor_copy(dst[:, :, :, 0:2], src[:, :, :, 0:2])
-                nc.scalar.copy(dst[:, :, :, 2:4], src[:, :, :, 2:4])
+            dst = b[:].rearrange("p (th tl m j) -> p th m j tl", th=2, tl=2, j=4)
+            src = w1_raw[e][:].rearrange("p j (m th tl) -> p th m j tl", th=2, tl=2)
+            if e >= E - SHARED:
+                nc.vector.tensor_copy(dst[:, 0], src[:, 0])
+                nc.scalar.copy(dst[:, 1], src[:, 1])
             elif e % 2 == 1:
                 nc.vector.tensor_copy(dst, src)
             else:
                 nc.scalar.copy(dst, src)
             st["w1b", e] = b
 
-        def quant_w1(e):
+        def layer1(e):
             q = ring.tile([P, H], U32, name="w1_q", align_bytes=64)
             s = ring.tile([P, H], U8, name="w1_s", align_bytes=64)
-            parts = 2 if e == E - 1 else 1
+            parts = 2 if e >= E - SHARED else 1
             w = H // parts
             for i in range(parts):
                 nc.vector.quantize_mx(
@@ -100,91 +104,105 @@ def tile_moe_pkd_mlp_silu_kernel(tc, x_words, x_scales, w1, w2, gate, offs, pos1
                     scales=s[:, i * w : (i + 1) * w],
                     in_=st["w1b", e][:, 4 * i * w : 4 * (i + 1) * w],
                 )
-            st["w1q", e] = (q, s)
-
-        def layer1(e):
-            q, s = st["w1q", e]
-            slots = slice((e % PAIR) * C, (e % PAIR + 1) * C)
+            g, c0 = divmod(e * C, GATHER)
             a = psum.tile([P, 4, C], F32, name="a")
             for t in range(4):
                 nc.tensor.matmul_mx(
                     out=a[:, t, :],
                     lhsT=q[:, t * P : (t + 1) * P].bitcast(FP8X4),
                     lhsT_scale=s[:, t * P : (t + 1) * P],
-                    rhs=gw[e // PAIR][:, slots].bitcast(FP8X4),
-                    rhs_scale=gs[e // PAIR][:, slots],
+                    rhs=gw[g][:, c0 : c0 + C].bitcast(FP8X4),
+                    rhs_scale=gs[g][:, c0 : c0 + C],
                     start=True,
                     stop=True,
                 )
             st["a", e] = a
 
-        def stage2(e):
-            host = min(e + 2 - e % 2, E - 2)
-            b = w1_raw[host][:, e - host + 2, :].bitcast(BF16)
-            nc.scalar.activation(
-                out=b[:, 0 : 4 * C].rearrange("p (s t) -> p s t", t=4), in_=st["a", e][:].rearrange("p t s -> p s t"), func=ACT.Silu
-            )
-            dst = b[:, 4 * C :].rearrange("p (c i j) -> p c j i", i=4, j=4)
-            src = w2_raw[e][:].rearrange("p j (c i) -> p c j i", i=4)
-            if e in (10, 11):
-                nc.vector.tensor_copy(dst, src)
-            else:
-                nc.scalar.copy(dst, src)
-            st["b2", e] = b
+        def h_stage(g):
+            if g == E // 2 - 1:
+                return w2_raw[0][:, 0].rearrange("p j n -> p (j n)").bitcast(BF16)
+            e = 2 * g + 2
+            return w1_raw[e if e < E - SHARED else E - 1][:, 0, :].bitcast(BF16)
 
-        def layer2(e):
-            q = ring.tile([P, C + N], U32, name="l2_q", align_bytes=64)
-            s = ring.tile([P, C + N], U8, name="l2_s", align_bytes=64)
-            nc.vector.quantize_mx(out=q[:].bitcast(FP8X4), scales=s[:], in_=st["b2", e])
-            if e % PAIR == 0:
-                st["yp"] = psum.tile([P, PAIR * C], F32, name="yp")
-            nc.tensor.matmul_mx(
-                out=st["yp"][:, (e % PAIR) * C : (e % PAIR + 1) * C],
-                lhsT=q[:, C:].bitcast(FP8X4),
-                lhsT_scale=s[:, C:],
-                rhs=q[:, :C].bitcast(FP8X4),
-                rhs_scale=s[:, :C],
-                start=True,
-                stop=True,
-            )
-            st["yp", e // PAIR] = st["yp"]
+        def silu(e):
+            b = h_stage(e // 2)[:, (e % 2) * 4 * C : (e % 2 + 1) * 4 * C]
+            nc.scalar.activation(out=b.rearrange("p (s t) -> p s t", t=4), in_=st["a", e][:].rearrange("p t s -> p s t"), func=ACT.Silu)
 
-        def y_out(g):
-            nc.vector.tensor_copy(y[:, g * PAIR * C : (g + 1) * PAIR * C], st["yp", g][:])
+        def quant_h(g):
+            nc.vector.quantize_mx(out=hq[g][:].bitcast(FP8X4), scales=hs[g][:], in_=h_stage(g))
 
-        for g in range(AHEAD):
+        def cast_w2(g):
+            z, v = W2_GROUPS[g], W2_VECTOR[g]
+            b = keep.tile([P, z * 4 * N], BF16, name="w2_bf%d" % g, align_bytes=64)
+            dst = b[:].rearrange("p (e c i j) -> p e c j i", e=z, i=4, j=4)
+            src = w2_raw[g][:].rearrange("p e j (c i) -> p e c j i", i=4)
+            if v > 0:
+                nc.vector.tensor_copy(dst[:, :v], src[:, :v])
+            if v < z:
+                nc.scalar.copy(dst[:, v:], src[:, v:])
+            st["w2b", g] = b
+
+        def layer2(g):
+            z = W2_GROUPS[g]
+            q = keep.tile([P, z * N], U32, name="w2_q%d" % g, align_bytes=64)
+            s = keep.tile([P, z * N], U8, name="w2_s%d" % g, align_bytes=64)
+            nc.vector.quantize_mx(out=q[:].bitcast(FP8X4), scales=s[:], in_=st["w2b", g][:])
+            for i in range(z):
+                e = starts[g] + i
+                if e in Y_STARTS:
+                    st["y0"] = e
+                    st["yp", e] = psum.tile([P, 4 * C], F32, name="yp")
+                yp, k = st["yp", st["y0"]], e - st["y0"]
+                slots = slice((e % 2) * C, (e % 2 + 1) * C)
+                nc.tensor.matmul_mx(
+                    out=yp[:, k * C : (k + 1) * C],
+                    lhsT=q[:, i * N : (i + 1) * N].bitcast(FP8X4),
+                    lhsT_scale=s[:, i * N : (i + 1) * N],
+                    rhs=hq[e // 2][:, slots].bitcast(FP8X4),
+                    rhs_scale=hs[e // 2][:, slots],
+                    start=True,
+                    stop=True,
+                )
+
+        for g in range(S // GATHER):
             gather(g)
-        for g in range(E // PAIR + 1):
-            e0, e1 = PAIR * g, PAIR * g + 1
-            if e0 < E:
-                cast_w1(e0)
-            if g >= 2:
-                y_out(g - 2)
-            if g >= 1:
-                stage2(e0 - 2)
-                stage2(e0 - 1)
-            if e0 < E:
-                quant_w1(e0)
-                layer1(e0)
-                cast_w1(e1)
-            if g >= 1:
-                layer2(e0 - 2)
-            if e0 < E:
-                quant_w1(e1)
-                layer1(e1)
-            if g >= 1:
-                layer2(e0 - 1)
-            if g + AHEAD < E // PAIR:
-                gather(g + AHEAD)
-        y_out(E // PAIR - 1)
+        for g in range(E // 2):
+            e0, e1 = 2 * g, 2 * g + 1
+            last = g == E // 2 - 1
+            cast_w1(e0)
+            if g >= 1 and not last:
+                silu(e0 - 2)
+                silu(e0 - 1)
+            layer1(e0)
+            cast_w1(e1)
+            if last:
+                silu(e0 - 2)
+                silu(e0 - 1)
+            if g >= 1 and not last:
+                quant_h(g - 1)
+            layer1(e1)
+        cast_w2(0)
+        silu(E - 2)
+        silu(E - 1)
+        quant_h(E // 2 - 2)
+        quant_h(E // 2 - 1)
+        for g in range(1, len(W2_GROUPS) + 1):
+            if g < len(W2_GROUPS):
+                cast_w2(g)
+            layer2(g - 1)
+        y = keep.tile([P, S], F32, name="y", tag="w2_raw%d" % 4, align_bytes=64)
+        for e0, e1 in zip(Y_STARTS, Y_STARTS[1:] + (E,)):
+            nc.scalar.copy(y[:, e0 * C : e1 * C], st["yp", e0][:, : (e1 - e0) * C])
 
-        for c in range(T // OUT_CHUNK):
-            tok = slice(c * OUT_CHUNK, (c + 1) * OUT_CHUNK)
-            cols = slice(c * OUT_CHUNK // 16, (c + 1) * OUT_CHUNK // 16)
-            pa = ring.tile([P, OUT_CHUNK], F32, name="pa")
-            pb = ring.tile([P, OUT_CHUNK], F32, name="pb")
-            po = ring.tile([P, OUT_CHUNK], F32, name="po")
-            nc.vector.tensor_tensor(pa[:], y[:].indirect(pos1_sb[:, cols]), gate_sb[0][:, tok], ALU.mult)
-            nc.vector.tensor_tensor(pb[:], y[:].indirect(pos2_sb[:, cols]), gate_sb[1][:, tok], ALU.mult)
+        t0 = 0
+        for i, w in enumerate(OUT_CHUNKS):
+            tok = slice(t0, t0 + w)
+            cols = slice(t0 // 16, (t0 + w) // 16)
+            pa = keep.tile([P, w], F32, name="pa%d" % t0)
+            pb = keep.tile([P, w], F32, name="pb%d" % t0)
+            po = keep.tile([P, w], F32, name="po%d" % t0)
+            nc.vector.tensor_tensor(pa[:], y[:].indirect(pos1_sb[:, cols]), gate_sb[i][:, 0, :], ALU.mult)
+            nc.vector.tensor_tensor(pb[:], y[:].indirect(pos2_sb[:, cols]), gate_sb[i][:, 1, :], ALU.mult)
             nc.vector.tensor_tensor(po[:], pa[:], pb[:], ALU.add)
             nc.sync.dma_start(out[:, tok], po[:])
+            t0 = t0 + w

@@ -19,9 +19,10 @@ ALU = mybir.AluOpType
 
 GATHER = 512
 W2_GROUPS = (2, 2, 2, 2, 2, 1, 1)
-W2_VECTOR = (2, 2, 2, 0, 0, 1, 1)
-SHARED = 2
+W2_VECTOR = (2, 2, 2, 0, 0, 1, 0)
+SHARED = (8, 10, 11)
 Y_STARTS = (0, 4, 8, 11)
+W1_GROUPS = (2, 2, 2, 2, 2, 1, 1)
 OUT_CHUNKS = (512, 256)
 
 
@@ -52,19 +53,20 @@ def tile_moe_pkd_mlp_silu_kernel(tc, x_words, x_scales, w1, w2, gate, offs, pos1
             )
 
         starts = [sum(W2_GROUPS[:g]) for g in range(len(W2_GROUPS))]
-        w1_raw = [keep.tile([P, 4, H], F32, name="w1_raw%d" % e, align_bytes=64) for e in range(E)]
+        w1_starts = [sum(W1_GROUPS[:g]) for g in range(len(W1_GROUPS))]
+        w1_tiles = [keep.tile([P, z, 4, H], F32, name="w1_raw%d" % g, align_bytes=64) for g, z in enumerate(W1_GROUPS)]
+        w1_raw = [w1_tiles[g][:, i] for g, z in enumerate(W1_GROUPS) for i in range(z)]
         w2_raw = [
             keep.tile([P, z, 4, N], F32, name="w2_raw%d" % g, tag="w2_raw%d" % g, align_bytes=64) for g, z in enumerate(W2_GROUPS)
         ]
         gate_sb = [keep.tile([P, 2, w], F32, name="gate_sb%d" % i) for i, w in enumerate(OUT_CHUNKS)]
 
-        for e in range(E):
-            nc.sync.dma_start(w1_raw[e][:], w1[e].rearrange("(p j) c -> p j c", j=4))
-            if e == 4:
-                nc.sync.dma_start(pos1_sb[:], pos1)
-                nc.sync.dma_start(pos2_sb[:], pos2)
+        for g, z in enumerate(W1_GROUPS):
+            nc.sync.dma_start(w1_tiles[g][:], w1[w1_starts[g] : w1_starts[g] + z].rearrange("e (p j) c -> p e j c", j=4))
         for g, z in enumerate(W2_GROUPS):
             nc.sync.dma_start(w2_raw[g][:], w2[starts[g] : starts[g] + z].rearrange("e (p j) n -> p e j n", j=4))
+        nc.sync.dma_start(pos1_sb[:], pos1)
+        nc.sync.dma_start(pos2_sb[:], pos2)
         for i, w in enumerate(OUT_CHUNKS):
             t0 = sum(OUT_CHUNKS[:i])
             nc.sync.dma_start(gate_sb[i][:], gate[:, :, t0 : t0 + w].rearrange("r p t -> p r t"))
@@ -83,8 +85,8 @@ def tile_moe_pkd_mlp_silu_kernel(tc, x_words, x_scales, w1, w2, gate, offs, pos1
         def cast_w1(e):
             b = ring.tile([P, 4 * H], BF16, name="w1_bf", align_bytes=64)
             dst = b[:].rearrange("p (th tl m j) -> p th m j tl", th=2, tl=2, j=4)
-            src = w1_raw[e][:].rearrange("p j (m th tl) -> p th m j tl", th=2, tl=2)
-            if e >= E - SHARED:
+            src = w1_raw[e].rearrange("p j (m th tl) -> p th m j tl", th=2, tl=2)
+            if e in SHARED:
                 nc.vector.tensor_copy(dst[:, 0], src[:, 0])
                 nc.scalar.copy(dst[:, 1], src[:, 1])
             elif e % 2 == 1:
@@ -96,7 +98,7 @@ def tile_moe_pkd_mlp_silu_kernel(tc, x_words, x_scales, w1, w2, gate, offs, pos1
         def layer1(e):
             q = ring.tile([P, H], U32, name="w1_q", align_bytes=64)
             s = ring.tile([P, H], U8, name="w1_s", align_bytes=64)
-            parts = 2 if e >= E - SHARED else 1
+            parts = 2 if e in SHARED else 1
             w = H // parts
             for i in range(parts):
                 nc.vector.quantize_mx(
@@ -122,7 +124,7 @@ def tile_moe_pkd_mlp_silu_kernel(tc, x_words, x_scales, w1, w2, gate, offs, pos1
             if g == E // 2 - 1:
                 return w2_raw[0][:, 0].rearrange("p j n -> p (j n)").bitcast(BF16)
             e = 2 * g + 2
-            return w1_raw[e if e < E - SHARED else E - 1][:, 0, :].bitcast(BF16)
+            return w1_raw[e if e < E - 2 else E - 1][:, 0, :].bitcast(BF16)
 
         def silu(e):
             b = h_stage(e // 2)[:, (e % 2) * 4 * C : (e % 2 + 1) * 4 * C]
@@ -190,9 +192,12 @@ def tile_moe_pkd_mlp_silu_kernel(tc, x_words, x_scales, w1, w2, gate, offs, pos1
             if g < len(W2_GROUPS):
                 cast_w2(g)
             layer2(g - 1)
-        y = keep.tile([P, S], F32, name="y", tag="w2_raw%d" % 4, align_bytes=64)
+        y = keep.tile([P, S], F32, name="y", tag="w2_raw%d" % 6, align_bytes=64)
         for e0, e1 in zip(Y_STARTS, Y_STARTS[1:] + (E,)):
-            nc.scalar.copy(y[:, e0 * C : e1 * C], st["yp", e0][:, : (e1 - e0) * C])
+            if e0 < 8:
+                nc.scalar.copy(y[:, e0 * C : e1 * C], st["yp", e0][:, : (e1 - e0) * C])
+            else:
+                nc.vector.tensor_copy(y[:, e0 * C : e1 * C], st["yp", e0][:, : (e1 - e0) * C])
 
         t0 = 0
         for i, w in enumerate(OUT_CHUNKS):

from contextlib import ExitStack

import concourse.mybir as mybir

K, T, E, C, H, N = 512, 768, 12, 128, 512, 128
S = E * C
P = 128
FLOPS = 2 * S * (K * H + H * N)

F32 = mybir.dt.float32
BF16 = mybir.dt.bfloat16
I32 = mybir.dt.int32
U32 = mybir.dt.uint32
U16 = mybir.dt.uint16
U8 = mybir.dt.uint8
FP8X4 = mybir.dt.float8_e4m3fn_x4
ACT = mybir.ActivationFunctionType
ALU = mybir.AluOpType

GATHER = 512
W2_GROUPS = (2, 2, 2, 2, 2, 1, 1)
W2_VECTOR = (2, 2, 2, 0, 0, 1, 0)
SHARED = (8, 10, 11)
Y_STARTS = (0, 4, 8, 11)
W1_GROUPS = (2, 2, 2, 2, 2, 1, 1)
OUT_CHUNKS = (512, 256)


def tile_moe_pkd_mlp_silu_kernel(tc, x_words, x_scales, w1, w2, gate, offs, pos1, pos2, out):
    nc = tc.nc
    with ExitStack() as ctx:
        keep = ctx.enter_context(tc.tile_pool(name="keep", bufs=1))
        ring = ctx.enter_context(tc.tile_pool(name="ring", bufs=4))
        psum = ctx.enter_context(tc.psum_pool(name="psum", bufs=4))

        offs_sb = keep.tile([P, S // 16], U16, name="offs_sb")
        pos1_sb = keep.tile([P, T // 16], U16, name="pos1_sb")
        pos2_sb = keep.tile([P, T // 16], U16, name="pos2_sb")
        xw = keep.tile([P, T], I32, name="xw", align_bytes=64)
        xs = keep.tile([P, T], U8, name="xs", align_bytes=64)
        warm = keep.tile([P, 8], F32, name="warm")
        warm_out = keep.tile([P, 8], F32, name="warm_out")
        nc.gpsimd.memset(warm[:], 0.0)
        nc.scalar.activation(out=warm_out[:], in_=warm[:], func=ACT.Silu)

        nc.sync.dma_start(offs_sb[:], offs)
        nc.sync.dma_start(xw[:], x_words[0].rearrange("p t r -> p (t r)").bitcast(I32))
        rows = x_scales[0].bitcast(I32)
        for q in range(4):
            nc.sync.dma_start(
                xs[32 * q : 32 * q + 32, :].bitcast(I32),
                rows[4 * q : 4 * q + 4, :].unsqueeze(0).to_broadcast([8, 4, T // 4]),
            )

        starts = [sum(W2_GROUPS[:g]) for g in range(len(W2_GROUPS))]
        w1_starts = [sum(W1_GROUPS[:g]) for g in range(len(W1_GROUPS))]
        w1_tiles = [keep.tile([P, z, 4, H], F32, name="w1_raw%d" % g, align_bytes=64) for g, z in enumerate(W1_GROUPS)]
        w1_raw = [w1_tiles[g][:, i] for g, z in enumerate(W1_GROUPS) for i in range(z)]
        w2_raw = [
            keep.tile([P, z, 4, N], F32, name="w2_raw%d" % g, tag="w2_raw%d" % g, align_bytes=64) for g, z in enumerate(W2_GROUPS)
        ]
        gate_sb = [keep.tile([P, 2, w], F32, name="gate_sb%d" % i) for i, w in enumerate(OUT_CHUNKS)]

        for g, z in enumerate(W1_GROUPS):
            nc.sync.dma_start(w1_tiles[g][:], w1[w1_starts[g] : w1_starts[g] + z].rearrange("e (p j) c -> p e j c", j=4))
        for g, z in enumerate(W2_GROUPS):
            nc.sync.dma_start(w2_raw[g][:], w2[starts[g] : starts[g] + z].rearrange("e (p j) n -> p e j n", j=4))
        nc.sync.dma_start(pos1_sb[:], pos1)
        nc.sync.dma_start(pos2_sb[:], pos2)
        for i, w in enumerate(OUT_CHUNKS):
            t0 = sum(OUT_CHUNKS[:i])
            nc.sync.dma_start(gate_sb[i][:], gate[:, :, t0 : t0 + w].rearrange("r p t -> p r t"))

        gw = [keep.tile([P, GATHER], U32, name="gw%d" % g, align_bytes=64) for g in range(S // GATHER)]
        gs = [keep.tile([P, GATHER], U8, name="gs%d" % g, align_bytes=64) for g in range(S // GATHER)]
        hq = [keep.tile([P, 2 * C], U32, name="hq%d" % g, align_bytes=64) for g in range(E // 2)]
        hs = [keep.tile([P, 2 * C], U8, name="hs%d" % g, align_bytes=64) for g in range(E // 2)]
        st = {}

        def gather(g):
            cols = slice(g * GATHER // 16, (g + 1) * GATHER // 16)
            nc.vector.tensor_copy(gw[g][:], xw[:].bitcast(U32).indirect(offs_sb[:, cols]))
            nc.vector.tensor_copy(gs[g][:], xs[:].indirect(offs_sb[:, cols]))

        def cast_w1(e):
            b = ring.tile([P, 4 * H], BF16, name="w1_bf", align_bytes=64)
            dst = b[:].rearrange("p (th tl m j) -> p th m j tl", th=2, tl=2, j=4)
            src = w1_raw[e].rearrange("p j (m th tl) -> p th m j tl", th=2, tl=2)
            if e in SHARED:
                nc.vector.tensor_copy(dst[:, 0], src[:, 0])
                nc.scalar.copy(dst[:, 1], src[:, 1])
            elif e % 2 == 1:
                nc.vector.tensor_copy(dst, src)
            else:
                nc.scalar.copy(dst, src)
            st["w1b", e] = b

        def layer1(e):
            q = ring.tile([P, H], U32, name="w1_q", align_bytes=64)
            s = ring.tile([P, H], U8, name="w1_s", align_bytes=64)
            parts = 2 if e in SHARED else 1
            w = H // parts
            for i in range(parts):
                nc.vector.quantize_mx(
                    out=q[:, i * w : (i + 1) * w].bitcast(FP8X4),
                    scales=s[:, i * w : (i + 1) * w],
                    in_=st["w1b", e][:, 4 * i * w : 4 * (i + 1) * w],
                )
            g, c0 = divmod(e * C, GATHER)
            a = psum.tile([P, 4, C], F32, name="a")
            for t in range(4):
                nc.tensor.matmul_mx(
                    out=a[:, t, :],
                    lhsT=q[:, t * P : (t + 1) * P].bitcast(FP8X4),
                    lhsT_scale=s[:, t * P : (t + 1) * P],
                    rhs=gw[g][:, c0 : c0 + C].bitcast(FP8X4),
                    rhs_scale=gs[g][:, c0 : c0 + C],
                    start=True,
                    stop=True,
                )
            st["a", e] = a

        def h_stage(g):
            if g == E // 2 - 1:
                return w2_raw[0][:, 0].rearrange("p j n -> p (j n)").bitcast(BF16)
            e = 2 * g + 2
            return w1_raw[e if e < E - 2 else E - 1][:, 0, :].bitcast(BF16)

        def silu(e):
            b = h_stage(e // 2)[:, (e % 2) * 4 * C : (e % 2 + 1) * 4 * C]
            nc.scalar.activation(out=b.rearrange("p (s t) -> p s t", t=4), in_=st["a", e][:].rearrange("p t s -> p s t"), func=ACT.Silu)

        def quant_h(g):
            nc.vector.quantize_mx(out=hq[g][:].bitcast(FP8X4), scales=hs[g][:], in_=h_stage(g))

        def cast_w2(g):
            z, v = W2_GROUPS[g], W2_VECTOR[g]
            b = keep.tile([P, z * 4 * N], BF16, name="w2_bf%d" % g, align_bytes=64)
            dst = b[:].rearrange("p (e c i j) -> p e c j i", e=z, i=4, j=4)
            src = w2_raw[g][:].rearrange("p e j (c i) -> p e c j i", i=4)
            if v > 0:
                nc.vector.tensor_copy(dst[:, :v], src[:, :v])
            if v < z:
                nc.scalar.copy(dst[:, v:], src[:, v:])
            st["w2b", g] = b

        def layer2(g):
            z = W2_GROUPS[g]
            q = keep.tile([P, z * N], U32, name="w2_q%d" % g, align_bytes=64)
            s = keep.tile([P, z * N], U8, name="w2_s%d" % g, align_bytes=64)
            nc.vector.quantize_mx(out=q[:].bitcast(FP8X4), scales=s[:], in_=st["w2b", g][:])
            for i in range(z):
                e = starts[g] + i
                if e in Y_STARTS:
                    st["y0"] = e
                    st["yp", e] = psum.tile([P, 4 * C], F32, name="yp")
                yp, k = st["yp", st["y0"]], e - st["y0"]
                slots = slice((e % 2) * C, (e % 2 + 1) * C)
                nc.tensor.matmul_mx(
                    out=yp[:, k * C : (k + 1) * C],
                    lhsT=q[:, i * N : (i + 1) * N].bitcast(FP8X4),
                    lhsT_scale=s[:, i * N : (i + 1) * N],
                    rhs=hq[e // 2][:, slots].bitcast(FP8X4),
                    rhs_scale=hs[e // 2][:, slots],
                    start=True,
                    stop=True,
                )

        for g in range(S // GATHER):
            gather(g)
        for g in range(E // 2):
            e0, e1 = 2 * g, 2 * g + 1
            last = g == E // 2 - 1
            cast_w1(e0)
            if g >= 1 and not last:
                silu(e0 - 2)
                silu(e0 - 1)
            layer1(e0)
            cast_w1(e1)
            if last:
                silu(e0 - 2)
                silu(e0 - 1)
            if g >= 1 and not last:
                quant_h(g - 1)
            layer1(e1)
        cast_w2(0)
        silu(E - 2)
        silu(E - 1)
        quant_h(E // 2 - 2)
        quant_h(E // 2 - 1)
        for g in range(1, len(W2_GROUPS) + 1):
            if g < len(W2_GROUPS):
                cast_w2(g)
            layer2(g - 1)
        y = keep.tile([P, S], F32, name="y", tag="w2_raw%d" % 6, align_bytes=64)
        for e0, e1 in zip(Y_STARTS, Y_STARTS[1:] + (E,)):
            if e0 < 8:
                nc.scalar.copy(y[:, e0 * C : e1 * C], st["yp", e0][:, : (e1 - e0) * C])
            else:
                nc.vector.tensor_copy(y[:, e0 * C : e1 * C], st["yp", e0][:, : (e1 - e0) * C])

        t0 = 0
        for i, w in enumerate(OUT_CHUNKS):
            tok = slice(t0, t0 + w)
            cols = slice(t0 // 16, (t0 + w) // 16)
            pa = keep.tile([P, w], F32, name="pa%d" % t0)
            pb = keep.tile([P, w], F32, name="pb%d" % t0)
            po = keep.tile([P, w], F32, name="po%d" % t0)
            nc.vector.tensor_tensor(pa[:], y[:].indirect(pos1_sb[:, cols]), gate_sb[i][:, 0, :], ALU.mult)
            nc.vector.tensor_tensor(pb[:], y[:].indirect(pos2_sb[:, cols]), gate_sb[i][:, 1, :], ALU.mult)
            nc.vector.tensor_tensor(po[:], pa[:], pb[:], ALU.add)
            nc.sync.dma_start(out[:, tok], po[:])
            t0 = t0 + w
